import numpy as np
import ml_dtypes


def mxq(x, axis, fmt="e4m3"):
    dtype, down = {"e4m3": (ml_dtypes.float8_e4m3fn, 7), "e5m2": (ml_dtypes.float8_e5m2, 14)}[fmt]
    v = np.moveaxis(np.asarray(x, np.float32).astype(ml_dtypes.bfloat16).astype(np.float64), axis, -1)
    blocks = v.reshape(v.shape[:-1] + (-1, 32))
    amax = np.abs(blocks).max(-1, keepdims=True)
    byte = np.maximum(np.where(amax > 0, np.frexp(amax)[1] - 1 + 127, 0) - down, 1)
    scale = np.exp2(byte - 127.0)
    codes = (blocks / scale).astype(np.float32).astype(dtype).astype(np.float64)
    return np.moveaxis((codes * scale).reshape(v.shape), -1, axis)


WIDE = False


def mx_kscale(k):
    if not WIDE:
        return np.ones(k)
    levels = np.array([10, -10, 5, -5, 0])
    if k % 512:
        return np.exp2(np.random.permutation(np.resize(levels, k // 32))).repeat(32)
    a = np.empty((k // 512, 16))
    for p in range(k // 512):
        a[p, :8] = np.random.permutation(np.resize(levels, 8))
        for g in range(8):
            far = levels[np.abs(levels - a[p, g]) >= 10]
            a[p, g + 8] = far[np.random.randint(len(far))]
    return np.exp2(a.ravel()).repeat(32)


def f64(x):
    return np.asarray(x).astype(np.float64)


def striped(idx):
    return np.tile(idx.reshape(-1, 16).T, (8, 1)).astype(np.uint16)


def unstriped(offs):
    return offs[:16].T.reshape(-1).astype(np.int64)


E2M1 = np.array([0.0, 0.5, 1.0, 1.5, 2.0, 3.0, 4.0, 6.0, -0.0, -0.5, -1.0, -1.5, -2.0, -3.0, -4.0, -6.0])


def pack_weight(w, fmt):
    k, n = w.shape
    w = f64(np.asarray(w, np.float32).astype(ml_dtypes.bfloat16)).reshape(k // 32, 32, n)
    amax = np.abs(w).max(1)
    if fmt == "e4m3":
        byte = np.frexp(amax)[1] - 1 + 127 - 7
    else:
        mant, ex = np.frexp(amax / 6.0)
        byte = np.where(mant > 0.5, ex, ex - 1) + 127
    byte = np.clip(np.where(amax > 0, byte, 1), 1, 254)
    scaled = (w * np.exp2(127.0 - byte)[:, None, :]).reshape(k, n).astype(np.float32)
    by_word = np.ascontiguousarray(scaled.reshape(k // 512, 128, 4, n).transpose(0, 1, 3, 2))
    if fmt == "e4m3":
        words = by_word.astype(ml_dtypes.float8_e4m3fn).view(np.uint8)
    else:
        c = by_word.astype(ml_dtypes.float4_e2m1fn).view(np.uint8) & 0xF
        words = (c[..., 0::2] | (c[..., 1::2] << 4)).reshape(k // 512, 128, 2 * n)
    return np.ascontiguousarray(words), np.ascontiguousarray(byte.astype(np.uint8).reshape(k // 512, 16, n))


def unpack_weight(words, scales, fmt):
    g, _, n = scales.shape
    words = np.ascontiguousarray(words).reshape(g, 128, n, -1)
    if fmt == "e4m3":
        vals = words.view(ml_dtypes.float8_e4m3fn).astype(np.float64)
    else:
        nib = np.empty((g, 128, n, 4), np.uint8)
        nib[..., 0::2] = words & 0xF
        nib[..., 1::2] = words >> 4
        vals = E2M1[nib]
    vals = vals * np.repeat(np.exp2(scales.astype(np.float64) - 127.0), 8, axis=1)[..., None]
    return vals.transpose(0, 1, 3, 2).reshape(g * 512, n)


def planes(y):
    n, m = y.shape
    v = y.astype(np.float32).astype(ml_dtypes.bfloat16).astype(np.float64).reshape(n // 32, 32, m)
    top = np.abs(v).max(1)
    byte = np.clip(np.where(top > 0, np.frexp(top)[1] - 1 + 127 - 7, 1), 1, 254)
    codes = (v * np.exp2(127.0 - byte)[:, None, :]).reshape(n, m).astype(np.float32).astype(ml_dtypes.float8_e4m3fn).view(np.uint8)
    words = codes.reshape(n // 512, 128, 4, m).transpose(0, 1, 3, 2)
    return np.ascontiguousarray(words), np.ascontiguousarray(byte.astype(np.uint8).reshape(n // 512, 16, m))


def gelu(v):
    return 0.5 * v * (1.0 + np.tanh(np.sqrt(2.0 / np.pi) * (v + 0.044715 * v**3)))


K, T, E, C, H, N, HOT = 512, 640, 10, 128, 512, 512, 3


def by_expert(wq, xq):
    return np.concatenate([wq[e].T @ xq[:, e * C:(e + 1) * C] for e in range(E)], axis=1)


def setup_inputs():
    n = np.random.standard_normal
    s = mx_kscale(K)
    u = mx_kscale(H)
    first = np.random.permutation(np.repeat(np.arange(E), T // E))
    second = (first + 1 + np.random.permutation(np.repeat(np.arange(E - 1), -(-T // (E - 1)))[:T])) % E
    while np.bincount(second, minlength=E).max() != T // E:
        load = np.bincount(second, minlength=E); hi, lo = int(load.argmax()), int(load.argmin())
        t = np.flatnonzero((second == hi) & (first != lo))[0]; second[t] = lo
    slot_token = np.empty(E * C, np.int64); pos = np.empty((2, T), np.int64); fill = np.zeros(E, np.int64)
    place = np.stack([np.random.permutation(C) for _ in range(E)])
    for r, deal in enumerate((first, second)):
        for t in np.random.permutation(T):
            e = deal[t]; j = e * C + place[e, fill[e]]; fill[e] += 1; slot_token[j] = t; pos[r, t] = j
    g = np.random.uniform(0.2, 0.8, T)
    x = pack_weight(n((K, T)) * s[:, None], "e4m3")
    w1h = [pack_weight(m, "e4m3") for m in n((HOT, K, H)) / np.sqrt(K) / s[None, :, None]]
    w3h = [pack_weight(m, "e4m3") for m in n((HOT, K, H)) / np.sqrt(K) / s[None, :, None] * u]
    w2h = [pack_weight(m, "e4m3") for m in n((HOT, H, N)) / np.sqrt(H) / u[None, :, None]]
    w1c = [pack_weight(m, "e2m1") for m in n((E - HOT, K, H)) / np.sqrt(K) / s[None, :, None]]
    w3c = [pack_weight(m, "e2m1") for m in n((E - HOT, K, H)) / np.sqrt(K) / s[None, :, None] * u]
    w2c = [pack_weight(m, "e2m1") for m in n((E - HOT, H, N)) / np.sqrt(H) / u[None, :, None]]
    return {
        "x_words": x[0],
        "x_scales": x[1],
        "w1h_words": np.stack([m[0] for m in w1h]),
        "w1h_scales": np.stack([m[1] for m in w1h]),
        "w3h_words": np.stack([m[0] for m in w3h]),
        "w3h_scales": np.stack([m[1] for m in w3h]),
        "w2h_words": np.stack([m[0] for m in w2h]),
        "w2h_scales": np.stack([m[1] for m in w2h]),
        "w1c_words": np.stack([m[0] for m in w1c]),
        "w1c_scales": np.stack([m[1] for m in w1c]),
        "w3c_words": np.stack([m[0] for m in w3c]),
        "w3c_scales": np.stack([m[1] for m in w3c]),
        "w2c_words": np.stack([m[0] for m in w2c]),
        "w2c_scales": np.stack([m[1] for m in w2c]),
        "gate": np.stack([np.tile(g, (128, 1)), np.tile(1.0 - g, (128, 1))]).astype(np.float32),
        "offs": striped(slot_token),
        "pos1": striped(pos[0]),
        "pos2": striped(pos[1]),
    }


def reference(x_words, x_scales, w1h_words, w1h_scales, w3h_words, w3h_scales, w2h_words, w2h_scales, w1c_words, w1c_scales, w3c_words, w3c_scales, w2c_words, w2c_scales, gate, offs, pos1, pos2):
    w1h = np.stack([unpack_weight(w1h_words[e], w1h_scales[e], "e4m3") for e in range(HOT)])
    w3h = np.stack([unpack_weight(w3h_words[e], w3h_scales[e], "e4m3") for e in range(HOT)])
    w2h = np.stack([unpack_weight(w2h_words[e], w2h_scales[e], "e4m3") for e in range(HOT)])
    w1c = np.stack([unpack_weight(w1c_words[e], w1c_scales[e], "e2m1") for e in range(E - HOT)])
    w3c = np.stack([unpack_weight(w3c_words[e], w3c_scales[e], "e2m1") for e in range(E - HOT)])
    w2c = np.stack([unpack_weight(w2c_words[e], w2c_scales[e], "e2m1") for e in range(E - HOT)])
    idx = unstriped(offs)
    xq = unpack_weight(x_words, x_scales, "e4m3")[:, idx]
    w1 = [*w1h, *w1c]
    w3 = [*w3h, *w3c]
    w2 = [*w2h, *w2c]
    h = gelu(by_expert(w1, xq)) * by_expert(w3, xq)
    y = by_expert(w2, mxq(h, 0, "e4m3"))
    out = sum(f64(gate[r, :1]) * y[:, unstriped(p)] for r, p in enumerate((pos1, pos2)))
    out_0 = out
    return (out_0,) + planes(out_0)

@@ -1,0 +1,267 @@
+from contextlib import ExitStack
+
+import concourse.mybir as mybir
+from concourse.masks import make_identity
+
+K, T, E, C, H, N, HOT = 512, 640, 10, 128, 512, 512, 3
+S = E * C
+FLOPS = 2 * S * (2 * K * H + H * N)
+
+F32 = mybir.dt.float32
+BF16 = mybir.dt.bfloat16
+I32 = mybir.dt.int32
+U32 = mybir.dt.uint32
+U16 = mybir.dt.uint16
+U8 = mybir.dt.uint8
+FP8X4 = mybir.dt.float8_e4m3fn_x4
+FP4X4 = mybir.dt.float4_e2m1fn_x4
+GELU = mybir.ActivationFunctionType.Gelu_apprx_tanh
+COPY = mybir.ActivationFunctionType.Copy
+MULT = mybir.AluOpType.mult
+
+P = 128
+PACK = 4
+TILES = T // P
+PIECE = 160
+W1_ROW, W3_ROW, W2_ROW = 4, 8, 12
+
+
+def tile_moe_hot_glu_gelu_kernel(
+    tc, x_words, x_scales, w1h_words, w1h_scales, w3h_words, w3h_scales, w2h_words, w2h_scales,
+    w1c_words, w1c_scales, w3c_words, w3c_scales, w2c_words, w2c_scales, gate, offs, pos1, pos2,
+    out_0, out_1, out_2,
+):
+    nc = tc.nc
+    with ExitStack() as ctx:
+        held = ctx.enter_context(tc.tile_pool(name="held", bufs=1))
+        ring = ctx.enter_context(tc.tile_pool(name="ring", bufs=2))
+        psum = ctx.enter_context(tc.psum_pool(name="psum", bufs=2))
+
+        def zeroed_plane(name, width, engine):
+            plane = held.tile([P, width], U8, name=name, align_bytes=64)
+            engine.memset(plane[:].bitcast(I32), 0)
+            return plane
+
+        def load_scales(plane, scales, row):
+            rows = scales.rearrange("e s b n -> b (e s) n").bitcast(I32)
+            view = plane[:].bitcast(I32).rearrange("p (e n) -> p e n", n=rows.shape[2])
+            for q in range(4):
+                nc.sync.dma_start(out=view[32 * q + row : 32 * q + row + 4], in_=rows[4 * q : 4 * q + 4])
+
+        words = {}
+
+        def load_words(name, hot_words, cold_words, first, last):
+            if first < HOT:
+                rows = hot_words.bitcast(I32)[first:last].rearrange("e s p n t -> p (e s) (n t)")
+            else:
+                rows = cold_words.bitcast(I32)[first - HOT : last - HOT].rearrange("e s p n -> p (e s) n")
+            loaded = held.tile([P, last - first, 4 * rows.shape[2]], U8, name=f"{name}_{first}", align_bytes=64)
+            nc.sync.dma_start(out=loaded[:].bitcast(I32), in_=rows)
+            for e in range(first, last):
+                words[name, e] = loaded[:, e - first, :]
+
+        x_plane = zeroed_plane("x_plane", T, nc.vector)
+        hot13 = zeroed_plane("hot13", HOT * H, nc.vector)
+        cold1 = zeroed_plane("cold1", (E - HOT) * H, nc.vector)
+        cold3 = zeroed_plane("cold3", (E - HOT) * H, nc.vector)
+        hot2 = zeroed_plane("hot2", HOT * N, nc.gpsimd)
+        cold2 = zeroed_plane("cold2", (E - HOT) * N, nc.gpsimd)
+        identity = held.tile([P, P], F32, name="identity")
+        make_identity(nc, identity[:])
+        gate_rows = held.tile([P, P], F32, name="gate_rows")
+        nc.gpsimd.memset(gate_rows[:], 0.0)
+
+        offs_sb = held.tile([P, S // 16], U16, name="offs_sb")
+        nc.sync.dma_start(offs_sb[:], offs)
+        x_sb = held.tile([P, T], I32, name="x_sb", align_bytes=64)
+        nc.sync.dma_start(out=x_sb[:], in_=x_words.rearrange("s p t d -> p (s t d)").bitcast(I32))
+        x_rows = x_scales.rearrange("s b t -> (s b) t").bitcast(I32)
+        for q in range(4):
+            nc.sync.dma_start(out=x_plane[:].bitcast(I32)[32 * q : 32 * q + 4], in_=x_rows[4 * q : 4 * q + 4])
+        load_words("w1", w1h_words, w1c_words, 0, 1)
+        load_words("w3", w3h_words, w3c_words, 0, 1)
+        load_scales(hot13, w1h_scales, W1_ROW)
+        load_scales(hot13, w3h_scales, W3_ROW)
+        load_words("w1", w1h_words, w1c_words, 1, 3)
+        load_words("w3", w3h_words, w3c_words, 1, 3)
+        load_scales(hot2, w2h_scales, W2_ROW)
+        load_scales(cold1, w1c_scales, 0)
+        load_scales(cold3, w3c_scales, 0)
+        load_words("w2", w2h_words, w2c_words, 0, 2)
+        load_words("w1", w1h_words, w1c_words, 3, 6)
+        load_words("w3", w3h_words, w3c_words, 3, 6)
+        load_words("w2", w2h_words, w2c_words, 2, 3)
+        load_scales(cold2, w2c_scales, 0)
+        load_words("w1", w1h_words, w1c_words, 6, 10)
+        load_words("w3", w3h_words, w3c_words, 6, 10)
+        load_words("w2", w2h_words, w2c_words, 3, 6)
+        load_words("w2", w2h_words, w2c_words, 6, 10)
+        pos_sb = []
+        for r, pos in enumerate((pos1, pos2)):
+            loaded = held.tile([P, T // 16], U16, name=f"pos_sb{r}")
+            nc.sync.dma_start(loaded[:], pos)
+            pos_sb.append(loaded)
+        for r in range(2):
+            nc.sync.dma_start(
+                out=gate_rows[TILES * r : TILES * (r + 1), :],
+                in_=gate[r, 0:1, :].rearrange("o (j p) -> (o j) p", p=P),
+            )
+
+        def weight(name, e, first, last):
+            hot_plane, hot_row, cold_plane = {
+                "w1": (hot13, W1_ROW, cold1), "w3": (hot13, W3_ROW, cold3), "w2": (hot2, W2_ROW, cold2),
+            }[name]
+            if e < HOT:
+                codes = words[name, e][:, 4 * first : 4 * last].bitcast(FP8X4)
+                return codes, hot_plane[hot_row:P, e * H + first : e * H + last]
+            codes = words[name, e][:, 2 * first : 2 * last].bitcast(FP4X4)
+            return codes, cold_plane[:, (e - HOT) * H + first : (e - HOT) * H + last]
+
+        y_sb = held.tile([P, N // P, S], F32, name="y_sb")
+        tokens = {}
+        hidden = {}
+        h_codes = {}
+
+        def gather_tokens(pair):
+            listed = offs_sb[:, 16 * pair : 16 * (pair + 1)]
+            codes = ring.tile([P, 2 * C], U32, name="slot_codes", align_bytes=64)
+            plane = ring.tile([P, 2 * C], U8, name="slot_plane", align_bytes=64)
+            nc.vector.tensor_copy(codes[:], x_sb[:].bitcast(U32).indirect(listed))
+            nc.vector.tensor_copy(plane[:], x_plane[:].indirect(listed))
+            tokens[pair] = (codes, plane)
+
+        def first_layer(e):
+            codes, plane = tokens[e // 2]
+            cols = slice(C * (e % 2), C * (e % 2 + 1))
+            sums = []
+            for name, tag in (("w1", "bank_a"), ("w3", "bank_b")):
+                bank = psum.tile([P, H], F32, name=tag)
+                w_codes, w_plane = weight(name, e, 0, H)
+                nc.tensor.matmul_mx(
+                    bank[:], lhsT=codes[:, cols].bitcast(FP8X4), lhsT_scale=plane[:, cols],
+                    rhs=w_codes, rhs_scale=w_plane, start=True, stop=True,
+                )
+                sums.append(bank[:].rearrange("s (p u d) -> s u p d", u=2, d=2))
+            gelu = ring.tile([P, 2, P, 2], F32, name="gelu")
+            nc.scalar.activation(gelu[:], sums[0], GELU)
+            h = ring.tile([P, 2, P, 2], BF16, name="h", bufs=4)
+            nc.vector.tensor_tensor(h[:], gelu[:], sums[1], MULT)
+            hidden[e] = h
+
+        def quantise_hidden(pair):
+            bank = psum.tile([P, 2, 2, C], F32, name="bank_t")
+            for i in range(2):
+                pairs = hidden[2 * pair + i][:].rearrange("s u p d -> s (u p d)").bitcast(F32)
+                for u in range(2):
+                    nc.tensor.transpose(bank[:, i, u, :], pairs[:, P * u : P * (u + 1)], identity[:])
+            grouped = ring.tile([P, 2 * C * PACK], BF16, name="grouped", align_bytes=64)
+            nc.scalar.copy(
+                grouped[:].bitcast(F32).rearrange("p (i s u) -> p i s u", i=2, u=2),
+                bank[:].rearrange("p i u s -> p i s u"),
+            )
+            codes = ring.tile([P, 2 * C], U32, name="h_codes", align_bytes=64)
+            plane = ring.tile([P, 2 * C], U8, name="h_plane", align_bytes=64)
+            nc.vector.quantize_mx(codes[:].bitcast(FP8X4), plane[:], grouped[:])
+            h_codes[pair] = (codes, plane)
+
+        def second_layer(e):
+            codes, plane = h_codes[e // 2]
+            cols = slice(C * (e % 2), C * (e % 2 + 1))
+            bank = psum.tile([P, N // P, C], F32, name="bank_y")
+            for c in range(N // P):
+                w_codes, w_plane = weight("w2", e, P * c, P * (c + 1))
+                nc.tensor.matmul_mx(
+                    bank[:, c, :], lhsT=w_codes, lhsT_scale=w_plane,
+                    rhs=codes[:, cols].bitcast(FP8X4), rhs_scale=plane[:, cols], start=True, stop=True,
+                )
+            if e == E - 1:
+                nc.vector.tensor_copy(y_sb[:, :, C * e : C * (e + 1)], bank[:])
+            else:
+                nc.scalar.copy(y_sb[:, :, C * e : C * (e + 1)], bank[:])
+
+        gather_tokens(0)
+        gather_tokens(1)
+        first_layer(0)
+        first_layer(1)
+        for pair in range(1, E // 2):
+            if pair + 1 < E // 2:
+                gather_tokens(pair + 1)
+            first_layer(2 * pair)
+            quantise_hidden(pair - 1)
+            first_layer(2 * pair + 1)
+            second_layer(2 * pair - 2)
+            second_layer(2 * pair - 1)
+        quantise_hidden(E // 2 - 1)
+        second_layer(E - 2)
+        second_layer(E - 1)
+
+        gate_bank = psum.tile([P, P], F32, name="bank_t")
+        nc.tensor.transpose(gate_bank[:], gate_rows[:], identity[:])
+        gate_cols = held.tile([P, 2 * TILES], F32, name="gate_cols")
+        nc.vector.tensor_copy(gate_cols[:], gate_bank[:, 0 : 2 * TILES])
+
+        picked = held.tile([P, 2, N // P, T], F32, name="picked")
+        result = held.tile([P, PACK, T], F32, name="result")
+        rounded = held.tile([P, T * PACK], BF16, name="rounded", align_bytes=64)
+        out_codes = held.tile([P, T], U32, name="out_codes", align_bytes=64)
+        out_plane = held.tile([P, T], U8, name="out_plane", align_bytes=64)
+        out_rows = out_0.rearrange("(p t) c -> p t c", t=PACK)
+        out_words = out_1.rearrange("s p c d -> p (s c d)").bitcast(I32)
+
+        def gather_results(piece):
+            for r in range(2):
+                listed = pos_sb[r][:, PIECE // 16 * piece : PIECE // 16 * (piece + 1)]
+                for c in range(N // P):
+                    nc.vector.tensor_copy(
+                        picked[:, r, c, PIECE * piece : PIECE * (piece + 1)], y_sb[:, c, :].indirect(listed)
+                    )
+
+        def combine(j):
+            last = j == TILES - 1
+            cols = slice(P * j, P * (j + 1))
+            gated = []
+            for r in range(2):
+                bank = psum.tile([P, N], F32, name="bank_t" if last else "bank_a")
+                for c in range(N // P):
+                    nc.tensor.transpose(bank[:, P * c : P * (c + 1)], picked[:, r, c, cols], identity[:])
+                product = ring.tile([P, PACK, P], F32, name="product", bufs=4)
+                dealt = bank[:].rearrange("s (p t) -> s t p", t=PACK)
+                g = gate_cols[:, TILES * r + j : TILES * r + j + 1]
+                if last and r == 1:
+                    nc.vector.tensor_scalar(product[:], dealt, g, None, MULT)
+                else:
+                    nc.scalar.activation(product[:], dealt, COPY, scale=g)
+                gated.append(product)
+            total = psum.tile([P, PACK, P], F32, name="bank_b")
+            for t in range(PACK):
+                for r in range(2):
+                    nc.tensor.matmul(
+                        total[:, t, :], lhsT=gated[r][:, t, :], rhs=identity[:],
+                        start=(r == 0), stop=(r == 1), is_transpose=True,
+                    )
+            woven = rounded[:, PACK * P * j : PACK * P * (j + 1)].rearrange("p (s t) -> p s t", t=PACK)
+            if last:
+                nc.vector.tensor_copy(result[:, :, cols], total[:])
+                nc.vector.tensor_copy(woven, result[:, :, cols].rearrange("p t s -> p s t"))
+            else:
+                nc.scalar.copy(result[:, :, cols], total[:])
+                nc.scalar.copy(woven, total[:].rearrange("p t s -> p s t"))
+            nc.sync.dma_start(out=out_rows[:, :, cols], in_=result[:, :, cols])
+
+        def hand_on(first, last):
+            cols = slice(P * first, P * last)
+            nc.vector.quantize_mx(
+                out_codes[:, cols].bitcast(FP8X4), out_plane[:, cols], rounded[:, PACK * P * first : PACK * P * last]
+            )
+            nc.sync.dma_start(out=out_words[:, cols], in_=out_codes[:, cols].bitcast(I32))
+
+        for piece in range(T // PIECE):
+            gather_results(piece)
+            combine(piece)
+        combine(TILES - 1)
+        hand_on(0, 2)
+        hand_on(2, 3)
+        hand_on(3, 5)
+        scale_rows = out_2.rearrange("s b c -> (s b) c").bitcast(I32)
+        for q in range(4):
+            nc.sync.dma_start(out=scale_rows[4 * q : 4 * q + 4], in_=out_plane[:].bitcast(I32)[32 * q : 32 * q + 4])

@@ -18,11 +18,19 @@ FP4X4 = mybir.dt.float4_e2m1fn_x4
 GELU = mybir.ActivationFunctionType.Gelu_apprx_tanh
 COPY = mybir.ActivationFunctionType.Copy
 MULT = mybir.AluOpType.mult
+ADD = mybir.AluOpType.add
 
 P = 128
 PACK = 4
 TILES = T // P
 PIECE = 160
+GATE_STEP = 26 * TILES + 1
+BANKS = ("a0", "a1", "b0", "b1", "t0", "t1", "y0", "y1")
+ORDER = list(range(HOT, E)) + list(range(HOT))
+GROUPS = [[0, 1], [2, 3], [4, 5], [6, 7], [8], [9]]
+Y_BANK = ["y0", "y1"] * 4 + ["a0", "b0"]
+FORWARD = [("a0", "a1")] * 4 + [("t0", "a0")]
+BACK = ["y0", "t0", "y1", "y0", "b0"]
 W1_ROW, W3_ROW, W2_ROW = 4, 8, 12
 
 
@@ -35,7 +43,9 @@ def tile_moe_hot_glu_gelu_kernel(
     with ExitStack() as ctx:
         held = ctx.enter_context(tc.tile_pool(name="held", bufs=1))
         ring = ctx.enter_context(tc.tile_pool(name="ring", bufs=2))
-        psum = ctx.enter_context(tc.psum_pool(name="psum", bufs=2))
+        psum = ctx.enter_context(tc.psum_pool(name="psum", bufs=1))
+
+        banks = {name: psum.tile([P, H], F32, name="bank_" + name) for name in BANKS}
 
         def zeroed_plane(name, width, engine):
             plane = held.tile([P, width], U8, name=name, align_bytes=64)
@@ -60,52 +70,56 @@ def tile_moe_hot_glu_gelu_kernel(
             for e in range(first, last):
                 words[name, e] = loaded[:, e - first, :]
 
-        x_plane = zeroed_plane("x_plane", T, nc.vector)
-        hot13 = zeroed_plane("hot13", HOT * H, nc.vector)
+        x_plane = zeroed_plane("x_plane", T, nc.gpsimd)
         cold1 = zeroed_plane("cold1", (E - HOT) * H, nc.vector)
         cold3 = zeroed_plane("cold3", (E - HOT) * H, nc.vector)
-        hot2 = zeroed_plane("hot2", HOT * N, nc.gpsimd)
+        gate_rows = held.tile([P, P], F32, name="gate_rows")
+        nc.gpsimd.memset(gate_rows[:], 0.0)
         cold2 = zeroed_plane("cold2", (E - HOT) * N, nc.gpsimd)
         identity = held.tile([P, P], F32, name="identity")
         make_identity(nc, identity[:])
-        gate_rows = held.tile([P, P], F32, name="gate_rows")
-        nc.gpsimd.memset(gate_rows[:], 0.0)
+        hot13 = zeroed_plane("hot13", HOT * H, nc.gpsimd)
+        hot2 = zeroed_plane("hot2", HOT * N, nc.gpsimd)
 
         offs_sb = held.tile([P, S // 16], U16, name="offs_sb")
-        nc.sync.dma_start(offs_sb[:], offs)
         x_sb = held.tile([P, T], I32, name="x_sb", align_bytes=64)
         nc.sync.dma_start(out=x_sb[:], in_=x_words.rearrange("s p t d -> p (s t d)").bitcast(I32))
         x_rows = x_scales.rearrange("s b t -> (s b) t").bitcast(I32)
         for q in range(4):
             nc.sync.dma_start(out=x_plane[:].bitcast(I32)[32 * q : 32 * q + 4], in_=x_rows[4 * q : 4 * q + 4])
-        load_words("w1", w1h_words, w1c_words, 0, 1)
-        load_words("w3", w3h_words, w3c_words, 0, 1)
-        load_scales(hot13, w1h_scales, W1_ROW)
-        load_scales(hot13, w3h_scales, W3_ROW)
-        load_words("w1", w1h_words, w1c_words, 1, 3)
-        load_words("w3", w3h_words, w3c_words, 1, 3)
-        load_scales(hot2, w2h_scales, W2_ROW)
+        nc.sync.dma_start(offs_sb[:], offs)
+
+        def load_first(first, last):
+            load_words("w1", w1h_words, w1c_words, first, last)
+            load_words("w3", w3h_words, w3c_words, first, last)
+
+        def load_second(first, last):
+            load_words("w2", w2h_words, w2c_words, first, last)
+
+        load_first(3, 5)
         load_scales(cold1, w1c_scales, 0)
         load_scales(cold3, w3c_scales, 0)
-        load_words("w2", w2h_words, w2c_words, 0, 2)
-        load_words("w1", w1h_words, w1c_words, 3, 6)
-        load_words("w3", w3h_words, w3c_words, 3, 6)
-        load_words("w2", w2h_words, w2c_words, 2, 3)
+        load_first(5, 8)
         load_scales(cold2, w2c_scales, 0)
-        load_words("w1", w1h_words, w1c_words, 6, 10)
-        load_words("w3", w3h_words, w3c_words, 6, 10)
-        load_words("w2", w2h_words, w2c_words, 3, 6)
-        load_words("w2", w2h_words, w2c_words, 6, 10)
+        load_scales(hot13, w1h_scales, W1_ROW)
+        load_scales(hot13, w3h_scales, W3_ROW)
+        load_first(8, 10)
+        load_second(3, 5)
+        load_first(0, 1)
+        load_second(5, 7)
+        load_first(1, 2)
+        load_first(2, 3)
+        load_second(7, 10)
         pos_sb = []
         for r, pos in enumerate((pos1, pos2)):
             loaded = held.tile([P, T // 16], U16, name=f"pos_sb{r}")
             nc.sync.dma_start(loaded[:], pos)
             pos_sb.append(loaded)
-        for r in range(2):
-            nc.sync.dma_start(
-                out=gate_rows[TILES * r : TILES * (r + 1), :],
-                in_=gate[r, 0:1, :].rearrange("o (j p) -> (o j) p", p=P),
-            )
+        chunks = gate.rearrange("r q (j p) -> (r q j) p", p=P)
+        nc.sync.dma_start(out=gate_rows[0 : 2 * TILES, :], in_=chunks[0 : 2 * P * TILES : GATE_STEP, :])
+        load_scales(hot2, w2h_scales, W2_ROW)
+        load_second(0, 2)
+        load_second(2, 3)
 
         def weight(name, e, first, last):
             hot_plane, hot_row, cold_plane = {
@@ -122,23 +136,25 @@ def tile_moe_hot_glu_gelu_kernel(
         hidden = {}
         h_codes = {}
 
-        def gather_tokens(pair):
-            listed = offs_sb[:, 16 * pair : 16 * (pair + 1)]
-            codes = ring.tile([P, 2 * C], U32, name="slot_codes", align_bytes=64)
-            plane = ring.tile([P, 2 * C], U8, name="slot_plane", align_bytes=64)
+        def gather_tokens(first, last):
+            listed = offs_sb[:, C // 16 * first : C // 16 * last]
+            codes = ring.tile([P, C * (last - first)], U32, name="slot_codes", align_bytes=64, bufs=3)
+            plane = ring.tile([P, C * (last - first)], U8, name="slot_plane", align_bytes=64, bufs=3)
             nc.vector.tensor_copy(codes[:], x_sb[:].bitcast(U32).indirect(listed))
             nc.vector.tensor_copy(plane[:], x_plane[:].indirect(listed))
-            tokens[pair] = (codes, plane)
+            for e in range(first, last):
+                cols = slice(C * (e - first), C * (e - first + 1))
+                tokens[e] = (codes[:, cols], plane[:, cols])
 
-        def first_layer(e):
-            codes, plane = tokens[e // 2]
-            cols = slice(C * (e % 2), C * (e % 2 + 1))
+        def first_layer(step):
+            e = ORDER[step]
+            codes, plane = tokens[e]
             sums = []
-            for name, tag in (("w1", "bank_a"), ("w3", "bank_b")):
-                bank = psum.tile([P, H], F32, name=tag)
+            for name, tag in (("w1", "a"), ("w3", "b")):
+                bank = banks[f"{tag}{step % 2}"]
                 w_codes, w_plane = weight(name, e, 0, H)
                 nc.tensor.matmul_mx(
-                    bank[:], lhsT=codes[:, cols].bitcast(FP8X4), lhsT_scale=plane[:, cols],
+                    bank[:], lhsT=codes.bitcast(FP8X4), lhsT_scale=plane,
                     rhs=w_codes, rhs_scale=w_plane, start=True, stop=True,
                 )
                 sums.append(bank[:].rearrange("s (p u d) -> s u p d", u=2, d=2))
@@ -146,57 +162,76 @@ def tile_moe_hot_glu_gelu_kernel(
             nc.scalar.activation(gelu[:], sums[0], GELU)
             h = ring.tile([P, 2, P, 2], BF16, name="h", bufs=4)
             nc.vector.tensor_tensor(h[:], gelu[:], sums[1], MULT)
-            hidden[e] = h
+            hidden[step] = h
 
-        def quantise_hidden(pair):
-            bank = psum.tile([P, 2, 2, C], F32, name="bank_t")
-            for i in range(2):
-                pairs = hidden[2 * pair + i][:].rearrange("s u p d -> s (u p d)").bitcast(F32)
+        def quantise_hidden(g):
+            group = GROUPS[g]
+            width = C * len(group)
+            bank = banks[f"t{g % 2}"][:, 0 : 2 * width].rearrange("p (i u s) -> p i u s", u=2, s=C)
+            for i, e in enumerate(group):
+                pairs = hidden[e][:].rearrange("s u p d -> s (u p d)").bitcast(F32)
                 for u in range(2):
                     nc.tensor.transpose(bank[:, i, u, :], pairs[:, P * u : P * (u + 1)], identity[:])
-            grouped = ring.tile([P, 2 * C * PACK], BF16, name="grouped", align_bytes=64)
+            grouped = ring.tile([P, width * PACK], BF16, name="grouped", align_bytes=64)
             nc.scalar.copy(
-                grouped[:].bitcast(F32).rearrange("p (i s u) -> p i s u", i=2, u=2),
-                bank[:].rearrange("p i u s -> p i s u"),
+                grouped[:].bitcast(F32).rearrange("p (i s u) -> p i s u", s=C, u=2),
+                bank.rearrange("p i u s -> p i s u"),
             )
-            codes = ring.tile([P, 2 * C], U32, name="h_codes", align_bytes=64)
-            plane = ring.tile([P, 2 * C], U8, name="h_plane", align_bytes=64)
+            codes = held.tile([P, width], U32, name=f"h_codes{g}", align_bytes=64)
+            plane = held.tile([P, width], U8, name=f"h_plane{g}", align_bytes=64)
             nc.vector.quantize_mx(codes[:].bitcast(FP8X4), plane[:], grouped[:])
-            h_codes[pair] = (codes, plane)
+            for i, e in enumerate(group):
+                h_codes[e] = (codes[:, C * i : C * (i + 1)], plane[:, C * i : C * (i + 1)])
 
-        def second_layer(e):
-            codes, plane = h_codes[e // 2]
-            cols = slice(C * (e % 2), C * (e % 2 + 1))
-            bank = psum.tile([P, N // P, C], F32, name="bank_y")
+        def second_layer(step):
+            e = ORDER[step]
+            codes, plane = h_codes[step]
+            bank = banks[Y_BANK[step]][:].rearrange("p (c s) -> p c s", s=C)
             for c in range(N // P):
                 w_codes, w_plane = weight("w2", e, P * c, P * (c + 1))
                 nc.tensor.matmul_mx(
                     bank[:, c, :], lhsT=w_codes, lhsT_scale=w_plane,
-                    rhs=codes[:, cols].bitcast(FP8X4), rhs_scale=plane[:, cols], start=True, stop=True,
+                    rhs=codes.bitcast(FP8X4), rhs_scale=plane, start=True, stop=True,
                 )
-            if e == E - 1:
-                nc.vector.tensor_copy(y_sb[:, :, C * e : C * (e + 1)], bank[:])
+            slots = slice(C * e, C * (e + 1))
+            if step % 2:
+                nc.vector.tensor_copy(y_sb[:, :, slots], bank)
             else:
-                nc.scalar.copy(y_sb[:, :, C * e : C * (e + 1)], bank[:])
+                nc.scalar.copy(y_sb[:, :, slots], bank)
 
-        gather_tokens(0)
-        gather_tokens(1)
+        gather_tokens(3, 5)
+        gather_tokens(5, 7)
+        gather_tokens(7, 10)
         first_layer(0)
         first_layer(1)
-        for pair in range(1, E // 2):
-            if pair + 1 < E // 2:
-                gather_tokens(pair + 1)
-            first_layer(2 * pair)
-            quantise_hidden(pair - 1)
-            first_layer(2 * pair + 1)
-            second_layer(2 * pair - 2)
-            second_layer(2 * pair - 1)
-        quantise_hidden(E // 2 - 1)
-        second_layer(E - 2)
-        second_layer(E - 1)
-
-        gate_bank = psum.tile([P, P], F32, name="bank_t")
-        nc.tensor.transpose(gate_bank[:], gate_rows[:], identity[:])
+        gather_tokens(0, 1)
+        first_layer(2)
+        quantise_hidden(0)
+        first_layer(3)
+        gather_tokens(1, 2)
+        first_layer(4)
+        quantise_hidden(1)
+        second_layer(0)
+        first_layer(5)
+        second_layer(1)
+        first_layer(6)
+        gather_tokens(2, 3)
+        quantise_hidden(2)
+        second_layer(2)
+        first_layer(7)
+        second_layer(3)
+        first_layer(8)
+        quantise_hidden(3)
+        second_layer(4)
+        first_layer(9)
+        second_layer(5)
+        quantise_hidden(4)
+        second_layer(6)
+        quantise_hidden(5)
+        for step in range(7, E):
+            second_layer(step)
+        gate_bank = banks["y1"]
+        nc.tensor.transpose(gate_bank[:, 0:P], gate_rows[:], identity[:])
         gate_cols = held.tile([P, 2 * TILES], F32, name="gate_cols")
         nc.vector.tensor_copy(gate_cols[:], gate_bank[:, 0 : 2 * TILES])
 
@@ -216,37 +251,67 @@ def tile_moe_hot_glu_gelu_kernel(
                         picked[:, r, c, PIECE * piece : PIECE * (piece + 1)], y_sb[:, c, :].indirect(listed)
                     )
 
-        def combine(j):
-            last = j == TILES - 1
-            cols = slice(P * j, P * (j + 1))
-            gated = []
-            for r in range(2):
-                bank = psum.tile([P, N], F32, name="bank_t" if last else "bank_a")
-                for c in range(N // P):
-                    nc.tensor.transpose(bank[:, P * c : P * (c + 1)], picked[:, r, c, cols], identity[:])
-                product = ring.tile([P, PACK, P], F32, name="product", bufs=4)
-                dealt = bank[:].rearrange("s (p t) -> s t p", t=PACK)
-                g = gate_cols[:, TILES * r + j : TILES * r + j + 1]
-                if last and r == 1:
-                    nc.vector.tensor_scalar(product[:], dealt, g, None, MULT)
-                else:
-                    nc.scalar.activation(product[:], dealt, COPY, scale=g)
-                gated.append(product)
-            total = psum.tile([P, PACK, P], F32, name="bank_b")
+        def turn(r, c, j, bank):
+            nc.tensor.transpose(bank[:, P * c : P * (c + 1)], picked[:, r, c, P * j : P * (j + 1)], identity[:])
+
+        def dealt(bank):
+            return bank[:].rearrange("s (p t) -> s t p", t=PACK)
+
+        def gate_of(r, j):
+            return gate_cols[:, TILES * r + j : TILES * r + j + 1]
+
+        def times_gate(r, j, bank):
+            product = ring.tile([P, PACK, P], F32, name="product", bufs=4)
+            nc.scalar.activation(product[:], dealt(bank), COPY, scale=gate_of(r, j))
+            return product
+
+        def woven(j):
+            return rounded[:, PACK * P * j : PACK * P * (j + 1)].rearrange("p (s t) -> p s t", t=PACK)
+
+        def weave(j):
+            nc.scalar.copy(woven(j), banks[BACK[j]][:].rearrange("p (t s) -> p s t", s=P))
+
+        def turn_back(j, terms):
+            total = banks[BACK[j]][:].rearrange("p (t s) -> p t s", s=P)
             for t in range(PACK):
-                for r in range(2):
+                for r, term in enumerate(terms):
                     nc.tensor.matmul(
-                        total[:, t, :], lhsT=gated[r][:, t, :], rhs=identity[:],
-                        start=(r == 0), stop=(r == 1), is_transpose=True,
+                        total[:, t, :], lhsT=term[:, t, :], rhs=identity[:],
+                        start=(r == 0), stop=(r == len(terms) - 1), is_transpose=True,
                     )
-            woven = rounded[:, PACK * P * j : PACK * P * (j + 1)].rearrange("p (s t) -> p s t", t=PACK)
-            if last:
-                nc.vector.tensor_copy(result[:, :, cols], total[:])
-                nc.vector.tensor_copy(woven, result[:, :, cols].rearrange("p t s -> p s t"))
+            cols = slice(P * j, P * (j + 1))
+            if j == TILES - 1:
+                nc.vector.tensor_copy(result[:, :, cols], total)
+                nc.vector.tensor_copy(woven(j), result[:, :, cols].rearrange("p t s -> p s t"))
             else:
-                nc.scalar.copy(result[:, :, cols], total[:])
-                nc.scalar.copy(woven, total[:].rearrange("p t s -> p s t"))
+                nc.scalar.copy(result[:, :, cols], total)
             nc.sync.dma_start(out=out_rows[:, :, cols], in_=result[:, :, cols])
+
+        def combine(j):
+            terms = []
+            for r in range(2):
+                bank = banks[FORWARD[j][r]]
+                for c in range(N // P):
+                    turn(r, c, j, bank)
+                terms.append(times_gate(r, j, bank))
+            if j > 0:
+                weave(j - 1)
+            turn_back(j, terms)
+
+        def combine_last(tiles):
+            for c in range(N // P):
+                for j in tiles:
+                    turn(0, c, j, banks[FORWARD[j][0]])
+            firsts = {j: times_gate(0, j, banks[FORWARD[j][0]]) for j in tiles}
+            weave(tiles[0] - 1)
+            for c in range(N // P):
+                for j in tiles:
+                    turn(1, c, j, banks[FORWARD[j][1]])
+            for j in tiles:
+                both = ring.tile([P, PACK, P], F32, name="both")
+                nc.vector.scalar_tensor_tensor(both[:], dealt(banks[FORWARD[j][1]]), gate_of(1, j), firsts[j][:], MULT, ADD)
+                turn_back(j, [both])
+            weave(tiles[0])
 
         def hand_on(first, last):
             cols = slice(P * first, P * last)
@@ -257,11 +322,12 @@ def tile_moe_hot_glu_gelu_kernel(
 
         for piece in range(T // PIECE):
             gather_results(piece)
-            combine(piece)
-        combine(TILES - 1)
+            if piece < TILES - 2:
+                combine(piece)
+        combine_last([TILES - 2, TILES - 1])
         hand_on(0, 2)
-        hand_on(2, 3)
-        hand_on(3, 5)
+        hand_on(2, 4)
+        hand_on(4, 5)
         scale_rows = out_2.rearrange("s b c -> (s b) c").bitcast(I32)
         for q in range(4):
             nc.sync.dma_start(out=scale_rows[4 * q : 4 * q + 4], in_=out_plane[:].bitcast(I32)[32 * q : 32 * q + 4])

@@ -56,7 +56,7 @@ def tile_moe_hot_glu_gelu_kernel(
             rows = scales.rearrange("e s b n -> b (e s) n").bitcast(I32)
             view = plane[:].bitcast(I32).rearrange("p (e n) -> p e n", n=rows.shape[2])
             for q in range(4):
-                nc.sync.dma_start(out=view[32 * q + row : 32 * q + row + 4], in_=rows[4 * q : 4 * q + 4])
+                nc.sync.dma_start(out=view[row + q : P : 32], in_=rows[q:16:4])
 
         words = {}
 
@@ -86,7 +86,7 @@ def tile_moe_hot_glu_gelu_kernel(
         nc.sync.dma_start(out=x_sb[:], in_=x_words.rearrange("s p t d -> p (s t d)").bitcast(I32))
         x_rows = x_scales.rearrange("s b t -> (s b) t").bitcast(I32)
         for q in range(4):
-            nc.sync.dma_start(out=x_plane[:].bitcast(I32)[32 * q : 32 * q + 4], in_=x_rows[4 * q : 4 * q + 4])
+            nc.sync.dma_start(out=x_plane[:].bitcast(I32)[q:P:32], in_=x_rows[q:16:4])
         nc.sync.dma_start(offs_sb[:], offs)
 
         def load_first(first, last):
@@ -261,7 +261,7 @@ def tile_moe_hot_glu_gelu_kernel(
             return gate_cols[:, TILES * r + j : TILES * r + j + 1]
 
         def times_gate(r, j, bank):
-            product = ring.tile([P, PACK, P], F32, name="product", bufs=4)
+            product = ring.tile([P, PACK, P], F32, name="product", bufs=6)
             nc.scalar.activation(product[:], dealt(bank), COPY, scale=gate_of(r, j))
             return product
 
@@ -296,17 +296,18 @@ def tile_moe_hot_glu_gelu_kernel(
                 terms.append(times_gate(r, j, bank))
             if j > 0:
                 weave(j - 1)
-            turn_back(j, terms)
+            return terms
 
-        def combine_last(tiles):
+        def combine_last(tiles, waiting):
             for c in range(N // P):
                 for j in tiles:
                     turn(0, c, j, banks[FORWARD[j][0]])
             firsts = {j: times_gate(0, j, banks[FORWARD[j][0]]) for j in tiles}
-            weave(tiles[0] - 1)
             for c in range(N // P):
                 for j in tiles:
                     turn(1, c, j, banks[FORWARD[j][1]])
+            turn_back(tiles[0] - 1, waiting)
+            weave(tiles[0] - 1)
             for j in tiles:
                 both = ring.tile([P, PACK, P], F32, name="both")
                 nc.vector.scalar_tensor_tensor(both[:], dealt(banks[FORWARD[j][1]]), gate_of(1, j), firsts[j][:], MULT, ADD)
@@ -323,11 +324,13 @@ def tile_moe_hot_glu_gelu_kernel(
         for piece in range(T // PIECE):
             gather_results(piece)
             if piece < TILES - 2:
-                combine(piece)
-        combine_last([TILES - 2, TILES - 1])
+                terms = combine(piece)
+            if piece < TILES - 3:
+                turn_back(piece, terms)
+        combine_last([TILES - 2, TILES - 1], terms)
         hand_on(0, 2)
         hand_on(2, 4)
         hand_on(4, 5)
         scale_rows = out_2.rearrange("s b c -> (s b) c").bitcast(I32)
         for q in range(4):
-            nc.sync.dma_start(out=scale_rows[4 * q : 4 * q + 4], in_=out_plane[:].bitcast(I32)[32 * q : 32 * q + 4])
+            nc.scalar.dma_start(out=scale_rows[q:16:4], in_=out_plane[:].bitcast(I32)[q:P:32])

from contextlib import ExitStack

import concourse.mybir as mybir
from concourse.masks import make_identity

K, T, E, C, H, N, HOT = 512, 640, 10, 128, 512, 512, 3
S = E * C
FLOPS = 2 * S * (2 * K * H + H * N)

F32 = mybir.dt.float32
BF16 = mybir.dt.bfloat16
I32 = mybir.dt.int32
U32 = mybir.dt.uint32
U16 = mybir.dt.uint16
U8 = mybir.dt.uint8
FP8X4 = mybir.dt.float8_e4m3fn_x4
FP4X4 = mybir.dt.float4_e2m1fn_x4
GELU = mybir.ActivationFunctionType.Gelu_apprx_tanh
COPY = mybir.ActivationFunctionType.Copy
MULT = mybir.AluOpType.mult
ADD = mybir.AluOpType.add

P = 128
PACK = 4
TILES = T // P
PIECE = 160
GATE_STEP = 26 * TILES + 1
BANKS = ("a0", "a1", "b0", "b1", "t0", "t1", "y0", "y1")
ORDER = list(range(HOT, E)) + list(range(HOT))
GROUPS = [[0, 1], [2, 3], [4, 5], [6, 7], [8], [9]]
Y_BANK = ["y0", "y1"] * 4 + ["a0", "b0"]
FORWARD = [("a0", "a1")] * 4 + [("t0", "a0")]
BACK = ["y0", "t0", "y1", "y0", "b0"]
W1_ROW, W3_ROW, W2_ROW = 4, 8, 12


def tile_moe_hot_glu_gelu_kernel(
    tc, x_words, x_scales, w1h_words, w1h_scales, w3h_words, w3h_scales, w2h_words, w2h_scales,
    w1c_words, w1c_scales, w3c_words, w3c_scales, w2c_words, w2c_scales, gate, offs, pos1, pos2,
    out_0, out_1, out_2,
):
    nc = tc.nc
    with ExitStack() as ctx:
        held = ctx.enter_context(tc.tile_pool(name="held", bufs=1))
        ring = ctx.enter_context(tc.tile_pool(name="ring", bufs=2))
        psum = ctx.enter_context(tc.psum_pool(name="psum", bufs=1))

        banks = {name: psum.tile([P, H], F32, name="bank_" + name) for name in BANKS}

        def zeroed_plane(name, width, engine):
            plane = held.tile([P, width], U8, name=name, align_bytes=64)
            engine.memset(plane[:].bitcast(I32), 0)
            return plane

        def load_scales(plane, scales, row):
            rows = scales.rearrange("e s b n -> b (e s) n").bitcast(I32)
            view = plane[:].bitcast(I32).rearrange("p (e n) -> p e n", n=rows.shape[2])
            for q in range(4):
                nc.sync.dma_start(out=view[row + q : P : 32], in_=rows[q:16:4])

        words = {}

        def load_words(name, hot_words, cold_words, first, last):
            if first < HOT:
                rows = hot_words.bitcast(I32)[first:last].rearrange("e s p n t -> p (e s) (n t)")
            else:
                rows = cold_words.bitcast(I32)[first - HOT : last - HOT].rearrange("e s p n -> p (e s) n")
            loaded = held.tile([P, last - first, 4 * rows.shape[2]], U8, name=f"{name}_{first}", align_bytes=64)
            nc.sync.dma_start(out=loaded[:].bitcast(I32), in_=rows)
            for e in range(first, last):
                words[name, e] = loaded[:, e - first, :]

        x_plane = zeroed_plane("x_plane", T, nc.gpsimd)
        cold1 = zeroed_plane("cold1", (E - HOT) * H, nc.vector)
        cold3 = zeroed_plane("cold3", (E - HOT) * H, nc.vector)
        gate_rows = held.tile([P, P], F32, name="gate_rows")
        nc.gpsimd.memset(gate_rows[:], 0.0)
        cold2 = zeroed_plane("cold2", (E - HOT) * N, nc.gpsimd)
        identity = held.tile([P, P], F32, name="identity")
        make_identity(nc, identity[:])
        hot13 = zeroed_plane("hot13", HOT * H, nc.gpsimd)
        hot2 = zeroed_plane("hot2", HOT * N, nc.gpsimd)

        offs_sb = held.tile([P, S // 16], U16, name="offs_sb")
        x_sb = held.tile([P, T], I32, name="x_sb", align_bytes=64)
        nc.sync.dma_start(out=x_sb[:], in_=x_words.rearrange("s p t d -> p (s t d)").bitcast(I32))
        x_rows = x_scales.rearrange("s b t -> (s b) t").bitcast(I32)
        for q in range(4):
            nc.sync.dma_start(out=x_plane[:].bitcast(I32)[q:P:32], in_=x_rows[q:16:4])
        nc.sync.dma_start(offs_sb[:], offs)

        def load_first(first, last):
            load_words("w1", w1h_words, w1c_words, first, last)
            load_words("w3", w3h_words, w3c_words, first, last)

        def load_second(first, last):
            load_words("w2", w2h_words, w2c_words, first, last)

        load_first(3, 5)
        load_scales(cold1, w1c_scales, 0)
        load_scales(cold3, w3c_scales, 0)
        load_first(5, 8)
        load_scales(cold2, w2c_scales, 0)
        load_scales(hot13, w1h_scales, W1_ROW)
        load_scales(hot13, w3h_scales, W3_ROW)
        load_first(8, 10)
        load_second(3, 5)
        load_first(0, 1)
        load_second(5, 7)
        load_first(1, 2)
        load_first(2, 3)
        load_second(7, 10)
        pos_sb = []
        for r, pos in enumerate((pos1, pos2)):
            loaded = held.tile([P, T // 16], U16, name=f"pos_sb{r}")
            nc.sync.dma_start(loaded[:], pos)
            pos_sb.append(loaded)
        chunks = gate.rearrange("r q (j p) -> (r q j) p", p=P)
        nc.sync.dma_start(out=gate_rows[0 : 2 * TILES, :], in_=chunks[0 : 2 * P * TILES : GATE_STEP, :])
        load_scales(hot2, w2h_scales, W2_ROW)
        load_second(0, 2)
        load_second(2, 3)

        def weight(name, e, first, last):
            hot_plane, hot_row, cold_plane = {
                "w1": (hot13, W1_ROW, cold1), "w3": (hot13, W3_ROW, cold3), "w2": (hot2, W2_ROW, cold2),
            }[name]
            if e < HOT:
                codes = words[name, e][:, 4 * first : 4 * last].bitcast(FP8X4)
                return codes, hot_plane[hot_row:P, e * H + first : e * H + last]
            codes = words[name, e][:, 2 * first : 2 * last].bitcast(FP4X4)
            return codes, cold_plane[:, (e - HOT) * H + first : (e - HOT) * H + last]

        y_sb = held.tile([P, N // P, S], F32, name="y_sb")
        tokens = {}
        hidden = {}
        h_codes = {}

        def gather_tokens(first, last):
            listed = offs_sb[:, C // 16 * first : C // 16 * last]
            codes = ring.tile([P, C * (last - first)], U32, name="slot_codes", align_bytes=64, bufs=3)
            plane = ring.tile([P, C * (last - first)], U8, name="slot_plane", align_bytes=64, bufs=3)
            nc.vector.tensor_copy(codes[:], x_sb[:].bitcast(U32).indirect(listed))
            nc.vector.tensor_copy(plane[:], x_plane[:].indirect(listed))
            for e in range(first, last):
                cols = slice(C * (e - first), C * (e - first + 1))
                tokens[e] = (codes[:, cols], plane[:, cols])

        def first_layer(step):
            e = ORDER[step]
            codes, plane = tokens[e]
            sums = []
            for name, tag in (("w1", "a"), ("w3", "b")):
                bank = banks[f"{tag}{step % 2}"]
                w_codes, w_plane = weight(name, e, 0, H)
                nc.tensor.matmul_mx(
                    bank[:], lhsT=codes.bitcast(FP8X4), lhsT_scale=plane,
                    rhs=w_codes, rhs_scale=w_plane, start=True, stop=True,
                )
                sums.append(bank[:].rearrange("s (p u d) -> s u p d", u=2, d=2))
            gelu = ring.tile([P, 2, P, 2], F32, name="gelu")
            nc.scalar.activation(gelu[:], sums[0], GELU)
            h = ring.tile([P, 2, P, 2], BF16, name="h", bufs=4)
            nc.vector.tensor_tensor(h[:], gelu[:], sums[1], MULT)
            hidden[step] = h

        def quantise_hidden(g):
            group = GROUPS[g]
            width = C * len(group)
            bank = banks[f"t{g % 2}"][:, 0 : 2 * width].rearrange("p (i u s) -> p i u s", u=2, s=C)
            for i, e in enumerate(group):
                pairs = hidden[e][:].rearrange("s u p d -> s (u p d)").bitcast(F32)
                for u in range(2):
                    nc.tensor.transpose(bank[:, i, u, :], pairs[:, P * u : P * (u + 1)], identity[:])
            grouped = ring.tile([P, width * PACK], BF16, name="grouped", align_bytes=64)
            nc.scalar.copy(
                grouped[:].bitcast(F32).rearrange("p (i s u) -> p i s u", s=C, u=2),
                bank.rearrange("p i u s -> p i s u"),
            )
            codes = held.tile([P, width], U32, name=f"h_codes{g}", align_bytes=64)
            plane = held.tile([P, width], U8, name=f"h_plane{g}", align_bytes=64)
            nc.vector.quantize_mx(codes[:].bitcast(FP8X4), plane[:], grouped[:])
            for i, e in enumerate(group):
                h_codes[e] = (codes[:, C * i : C * (i + 1)], plane[:, C * i : C * (i + 1)])

        def second_layer(step):
            e = ORDER[step]
            codes, plane = h_codes[step]
            bank = banks[Y_BANK[step]][:].rearrange("p (c s) -> p c s", s=C)
            for c in range(N // P):
                w_codes, w_plane = weight("w2", e, P * c, P * (c + 1))
                nc.tensor.matmul_mx(
                    bank[:, c, :], lhsT=w_codes, lhsT_scale=w_plane,
                    rhs=codes.bitcast(FP8X4), rhs_scale=plane, start=True, stop=True,
                )
            slots = slice(C * e, C * (e + 1))
            if step % 2:
                nc.vector.tensor_copy(y_sb[:, :, slots], bank)
            else:
                nc.scalar.copy(y_sb[:, :, slots], bank)

        gather_tokens(3, 5)
        gather_tokens(5, 7)
        gather_tokens(7, 10)
        first_layer(0)
        first_layer(1)
        gather_tokens(0, 1)
        first_layer(2)
        quantise_hidden(0)
        first_layer(3)
        gather_tokens(1, 2)
        first_layer(4)
        quantise_hidden(1)
        second_layer(0)
        first_layer(5)
        second_layer(1)
        first_layer(6)
        gather_tokens(2, 3)
        quantise_hidden(2)
        second_layer(2)
        first_layer(7)
        second_layer(3)
        first_layer(8)
        quantise_hidden(3)
        second_layer(4)
        first_layer(9)
        second_layer(5)
        quantise_hidden(4)
        second_layer(6)
        quantise_hidden(5)
        for step in range(7, E):
            second_layer(step)
        gate_bank = banks["y1"]
        nc.tensor.transpose(gate_bank[:, 0:P], gate_rows[:], identity[:])
        gate_cols = held.tile([P, 2 * TILES], F32, name="gate_cols")
        nc.vector.tensor_copy(gate_cols[:], gate_bank[:, 0 : 2 * TILES])

        picked = held.tile([P, 2, N // P, T], F32, name="picked")
        result = held.tile([P, PACK, T], F32, name="result")
        rounded = held.tile([P, T * PACK], BF16, name="rounded", align_bytes=64)
        out_codes = held.tile([P, T], U32, name="out_codes", align_bytes=64)
        out_plane = held.tile([P, T], U8, name="out_plane", align_bytes=64)
        out_rows = out_0.rearrange("(p t) c -> p t c", t=PACK)
        out_words = out_1.rearrange("s p c d -> p (s c d)").bitcast(I32)

        def gather_results(piece):
            for r in range(2):
                listed = pos_sb[r][:, PIECE // 16 * piece : PIECE // 16 * (piece + 1)]
                for c in range(N // P):
                    nc.vector.tensor_copy(
                        picked[:, r, c, PIECE * piece : PIECE * (piece + 1)], y_sb[:, c, :].indirect(listed)
                    )

        def turn(r, c, j, bank):
            nc.tensor.transpose(bank[:, P * c : P * (c + 1)], picked[:, r, c, P * j : P * (j + 1)], identity[:])

        def dealt(bank):
            return bank[:].rearrange("s (p t) -> s t p", t=PACK)

        def gate_of(r, j):
            return gate_cols[:, TILES * r + j : TILES * r + j + 1]

        def times_gate(r, j, bank):
            product = ring.tile([P, PACK, P], F32, name="product", bufs=6)
            nc.scalar.activation(product[:], dealt(bank), COPY, scale=gate_of(r, j))
            return product

        def woven(j):
            return rounded[:, PACK * P * j : PACK * P * (j + 1)].rearrange("p (s t) -> p s t", t=PACK)

        def weave(j):
            nc.scalar.copy(woven(j), banks[BACK[j]][:].rearrange("p (t s) -> p s t", s=P))

        def turn_back(j, terms):
            total = banks[BACK[j]][:].rearrange("p (t s) -> p t s", s=P)
            for t in range(PACK):
                for r, term in enumerate(terms):
                    nc.tensor.matmul(
                        total[:, t, :], lhsT=term[:, t, :], rhs=identity[:],
                        start=(r == 0), stop=(r == len(terms) - 1), is_transpose=True,
                    )
            cols = slice(P * j, P * (j + 1))
            if j == TILES - 1:
                nc.vector.tensor_copy(result[:, :, cols], total)
                nc.vector.tensor_copy(woven(j), result[:, :, cols].rearrange("p t s -> p s t"))
            else:
                nc.scalar.copy(result[:, :, cols], total)
            nc.sync.dma_start(out=out_rows[:, :, cols], in_=result[:, :, cols])

        def combine(j):
            terms = []
            for r in range(2):
                bank = banks[FORWARD[j][r]]
                for c in range(N // P):
                    turn(r, c, j, bank)
                terms.append(times_gate(r, j, bank))
            if j > 0:
                weave(j - 1)
            return terms

        def combine_last(tiles, waiting):
            for c in range(N // P):
                for j in tiles:
                    turn(0, c, j, banks[FORWARD[j][0]])
            firsts = {j: times_gate(0, j, banks[FORWARD[j][0]]) for j in tiles}
            for c in range(N // P):
                for j in tiles:
                    turn(1, c, j, banks[FORWARD[j][1]])
            turn_back(tiles[0] - 1, waiting)
            weave(tiles[0] - 1)
            for j in tiles:
                both = ring.tile([P, PACK, P], F32, name="both")
                nc.vector.scalar_tensor_tensor(both[:], dealt(banks[FORWARD[j][1]]), gate_of(1, j), firsts[j][:], MULT, ADD)
                turn_back(j, [both])
            weave(tiles[0])

        def hand_on(first, last):
            cols = slice(P * first, P * last)
            nc.vector.quantize_mx(
                out_codes[:, cols].bitcast(FP8X4), out_plane[:, cols], rounded[:, PACK * P * first : PACK * P * last]
            )
            nc.sync.dma_start(out=out_words[:, cols], in_=out_codes[:, cols].bitcast(I32))

        for piece in range(T // PIECE):
            gather_results(piece)
            if piece < TILES - 2:
                terms = combine(piece)
            if piece < TILES - 3:
                turn_back(piece, terms)
        combine_last([TILES - 2, TILES - 1], terms)
        hand_on(0, 2)
        hand_on(2, 4)
        hand_on(4, 5)
        scale_rows = out_2.rearrange("s b c -> (s b) c").bitcast(I32)
        for q in range(4):
            nc.scalar.dma_start(out=scale_rows[q:16:4], in_=out_plane[:].bitcast(I32)[q:P:32])
